import numpy as np
import ml_dtypes


def mxq(x, axis, fmt="e4m3"):
    dtype, down = {"e4m3": (ml_dtypes.float8_e4m3fn, 7), "e5m2": (ml_dtypes.float8_e5m2, 14)}[fmt]
    v = np.moveaxis(np.asarray(x, np.float32).astype(ml_dtypes.bfloat16).astype(np.float64), axis, -1)
    blocks = v.reshape(v.shape[:-1] + (-1, 32))
    amax = np.abs(blocks).max(-1, keepdims=True)
    byte = np.maximum(np.where(amax > 0, np.frexp(amax)[1] - 1 + 127, 0) - down, 1)
    scale = np.exp2(byte - 127.0)
    codes = (blocks / scale).astype(np.float32).astype(dtype).astype(np.float64)
    return np.moveaxis((codes * scale).reshape(v.shape), -1, axis)


WIDE = False


def mx_kscale(k):
    if not WIDE:
        return np.ones(k)
    levels = np.array([10, -10, 5, -5, 0])
    if k % 512:
        return np.exp2(np.random.permutation(np.resize(levels, k // 32))).repeat(32)
    a = np.empty((k // 512, 16))
    for p in range(k // 512):
        a[p, :8] = np.random.permutation(np.resize(levels, 8))
        for g in range(8):
            far = levels[np.abs(levels - a[p, g]) >= 10]
            a[p, g + 8] = far[np.random.randint(len(far))]
    return np.exp2(a.ravel()).repeat(32)


def f64(x):
    return np.asarray(x).astype(np.float64)


def striped(idx):
    return np.tile(idx.reshape(-1, 16).T, (8, 1)).astype(np.uint16)


def unstriped(offs):
    return offs[:16].T.reshape(-1).astype(np.int64)


E2M1 = np.array([0.0, 0.5, 1.0, 1.5, 2.0, 3.0, 4.0, 6.0, -0.0, -0.5, -1.0, -1.5, -2.0, -3.0, -4.0, -6.0])


def pack_weight(w, fmt):
    k, n = w.shape
    w = f64(np.asarray(w, np.float32).astype(ml_dtypes.bfloat16)).reshape(k // 32, 32, n)
    amax = np.abs(w).max(1)
    if fmt == "e4m3":
        byte = np.frexp(amax)[1] - 1 + 127 - 7
    else:
        mant, ex = np.frexp(amax / 6.0)
        byte = np.where(mant > 0.5, ex, ex - 1) + 127
    byte = np.clip(np.where(amax > 0, byte, 1), 1, 254)
    scaled = (w * np.exp2(127.0 - byte)[:, None, :]).reshape(k, n).astype(np.float32)
    by_word = np.ascontiguousarray(scaled.reshape(k // 512, 128, 4, n).transpose(0, 1, 3, 2))
    if fmt == "e4m3":
        words = by_word.astype(ml_dtypes.float8_e4m3fn).view(np.uint8)
    else:
        c = by_word.astype(ml_dtypes.float4_e2m1fn).view(np.uint8) & 0xF
        words = (c[..., 0::2] | (c[..., 1::2] << 4)).reshape(k // 512, 128, 2 * n)
    return np.ascontiguousarray(words), np.ascontiguousarray(byte.astype(np.uint8).reshape(k // 512, 16, n))


def unpack_weight(words, scales, fmt):
    g, _, n = scales.shape
    words = np.ascontiguousarray(words).reshape(g, 128, n, -1)
    if fmt == "e4m3":
        vals = words.view(ml_dtypes.float8_e4m3fn).astype(np.float64)
    else:
        nib = np.empty((g, 128, n, 4), np.uint8)
        nib[..., 0::2] = words & 0xF
        nib[..., 1::2] = words >> 4
        vals = E2M1[nib]
    vals = vals * np.repeat(np.exp2(scales.astype(np.float64) - 127.0), 8, axis=1)[..., None]
    return vals.transpose(0, 1, 3, 2).reshape(g * 512, n)


def gelu(v):
    return 0.5 * v * (1.0 + np.tanh(np.sqrt(2.0 / np.pi) * (v + 0.044715 * v**3)))


def striped8(idx):
    return np.concatenate([v.reshape(-1, 16).T for v in idx]).astype(np.uint16)


def unstriped8(offs):
    return np.stack([offs[16 * g:16 * g + 16].T.reshape(-1) for g in range(8)]).astype(np.int64)


def heads(h, wgt, idx8):
    r = np.arange(h.shape[0])
    return wgt[r // 4 % 128] * h[r[:, None], idx8[r % 512 // 64]]


def put_heads(h, wgs, idx8, t2):
    r = np.arange(h.shape[0])
    page = np.zeros((h.shape[0], t2))
    page[r[:, None], idx8[r % 512 // 64]] = wgs[r // 4 % 128] * h
    return page


K, T, S, P, T2, H, N = 1024, 4096, 1024, 512, 1024, 512, 1024

def setup_inputs():
    n = np.random.standard_normal
    s, u = mx_kscale(K)[:, None], mx_kscale(H)[:, None]
    d = {}
    d["tab_words"], d["tab_scales"] = pack_weight(n((K, T)) * s, "e4m3")
    d["offs"] = striped(np.random.permutation(T)[:S])
    d["offs2"] = striped8(np.stack([np.random.permutation(S)[:P] for _ in range(8)]))
    d["offs3"] = striped8(np.stack([np.random.permutation(T2)[:P] for _ in range(8)]))
    d["w1"] = (0.55 * n((K, H)) / K**0.5 / s).astype(np.float32)
    d["w2"] = (3.0 * n((K, H)) / K**0.5 / s * u.T).astype(np.float32)
    d["w3_words"], d["w3_scales"] = pack_weight(1.2 * n((K, H)) / K**0.5 / s * u.T, "e4m3")
    d["wgt"] = np.repeat(np.random.uniform(0.5, 2.0, (8, P)), 16, axis=0).astype(np.float32)
    d["bias"] = (0.9 * n(H) * u[:, 0]).astype(np.float32)
    d["w4_words"], d["w4_scales"] = pack_weight(2.0 * n((H, N)) / H**0.5 / u, "e2m1")
    d["ref"] = (2.0 * n((N, P))).astype(np.float32)
    d["wgo"] = np.repeat(np.random.uniform(0.5, 2.0, (8, P)), 16, axis=0).astype(np.float32)
    return d

def reference(tab_words, tab_scales, offs, offs2, offs3, w1, w2, w3_words, w3_scales, wgt, bias, w4_words, w4_scales, ref, wgo):
    v = unpack_weight(tab_words, tab_scales, "e4m3")[:, unstriped(offs)]
    w3 = unpack_weight(w3_words, w3_scales, "e4m3")
    w4 = unpack_weight(w4_words, w4_scales, "e2m1")
    phase = mxq(f64(w1), 0, "e4m3").T @ v
    b = mxq(f64(w2), 0, "e4m3").T @ v
    d = w3.T @ v
    h = np.maximum(np.sin(phase) * b, np.cos(phase) * d)
    x = heads(h, f64(wgt), unstriped8(offs2)) + f64(bias)[:, None]
    e = (w4.T @ mxq(x, 0, "e4m3")) - f64(ref)
    y = np.sqrt(np.abs(e) + 1.0)
    return put_heads(y, f64(wgo), unstriped8(offs3), T2)

@@ -1,0 +1,251 @@
+import math
+from contextlib import ExitStack
+
+import concourse.mybir as mybir
+from concourse.masks import make_identity
+
+K, T, S, M, T2, H, N = 1024, 4096, 1024, 512, 1024, 512, 1024
+FLOPS = 2 * (3 * K * H * S + H * N * M)
+
+F32 = mybir.dt.float32
+BF16 = mybir.dt.bfloat16
+I32 = mybir.dt.int32
+U32 = mybir.dt.uint32
+U16 = mybir.dt.uint16
+U8 = mybir.dt.uint8
+FP8X4 = mybir.dt.float8_e4m3fn_x4
+FP4X4 = mybir.dt.float4_e2m1fn_x4
+ACT = mybir.ActivationFunctionType
+ALU = mybir.AluOpType
+
+P = 128
+PACK = 4
+K_PASS = P * PACK
+PASSES = K // K_PASS
+BANK = 512
+HALVES = S // BANK
+OUT_TILES = N // P
+DIRECT_TILES = 2
+KIB = 1024
+AHEAD = 2
+UNITS = PACK * HALVES
+
+
+def tile_list_spirometry_obstruction_slots_kernel(
+    tc, tab_words, tab_scales, offs, offs2, offs3, w1, w2, w3_words, w3_scales, wgt, bias,
+    w4_words, w4_scales, ref, wgo, out,
+):
+    nc = tc.nc
+    with ExitStack() as ctx:
+        keep = ctx.enter_context(tc.tile_pool(name="keep", bufs=1))
+        raw_pool = ctx.enter_context(tc.tile_pool(name="raw", bufs=4))
+        bf_pool = ctx.enter_context(tc.tile_pool(name="bf", bufs=2))
+        stage = ctx.enter_context(tc.tile_pool(name="stage", bufs=1))
+        work = ctx.enter_context(tc.tile_pool(name="work", bufs=3))
+        cos_pool = ctx.enter_context(tc.tile_pool(name="cosd", bufs=4))
+        psum_a = ctx.enter_context(tc.psum_pool(name="psum_a", bufs=3))
+        psum_b = ctx.enter_context(tc.psum_pool(name="psum_b", bufs=3))
+        psum_c = ctx.enter_context(tc.psum_pool(name="psum_c", bufs=2))
+
+        tab_sc = stage.tile([P, T], U8, name="tab_sc", align_bytes=64, offset=32 * KIB)
+        w3_sc_raw = keep.tile([P, H], U8, name="w3_sc_raw", align_bytes=64)
+        w4_sc_raw = keep.tile([P, N], U8, name="w4_sc_raw", align_bytes=64)
+        for plane in (tab_sc, w4_sc_raw, w3_sc_raw):
+            nc.vector.memset(plane[:].bitcast(I32), 0)
+
+        list1 = keep.tile([P, S // 16], U16, name="list1")
+        nc.sync.dma_start(list1[:], offs)
+        w4_raw = keep.tile([P, 2 * N], U8, name="w4_raw", align_bytes=64)
+        nc.sync.dma_start(w4_raw[:].bitcast(I32), w4_words[0].bitcast(I32))
+        tab = []
+        for a in range(PASSES):
+            tile = stage.tile([P, T], U32, name="tab%d" % a, align_bytes=64, offset=16 * KIB * a)
+            nc.sync.dma_start(tile[:].bitcast(I32), tab_words[a].rearrange("p t i -> p (t i)").bitcast(I32))
+            tab.append(tile)
+
+        def load_raw(w, a):
+            tile = raw_pool.tile([P, PACK, H], F32, name="raw")
+            nc.sync.dma_start(tile[:], w[a * K_PASS : (a + 1) * K_PASS, :].rearrange("(p j) c -> p j c", j=PACK))
+            return tile
+
+        w1_raw = [load_raw(w1, a) for a in range(PASSES)]
+        w3_raw = keep.tile([P, PASSES, H], I32, name="w3_raw", align_bytes=64)
+        nc.sync.dma_start(w3_raw[:], w3_words.rearrange("a p c i -> p a (c i)").bitcast(I32))
+        w2_raw = [load_raw(w2, a) for a in range(PASSES)]
+
+        for q in range(4):
+            nc.gpsimd.dma_start(tab_sc[32 * q : 32 * q + 4 * PASSES, :].bitcast(I32),
+                                tab_scales[:, 4 * q : 4 * q + 4, :].bitcast(I32))
+        for q in range(4):
+            nc.gpsimd.dma_start(w4_sc_raw[32 * q : 32 * q + 4, :].bitcast(I32),
+                                w4_scales[0, 4 * q : 4 * q + 4, :].bitcast(I32))
+        for q in range(4):
+            nc.gpsimd.dma_start(w3_sc_raw[32 * q : 32 * q + 4 * PASSES, :].bitcast(I32),
+                                w3_scales[:, 4 * q : 4 * q + 4, :].bitcast(I32))
+
+        list2 = keep.tile([P, M // 16], U16, name="list2")
+        nc.sync.dma_start(list2[:], offs2)
+        wgt_sb = keep.tile([P, M], F32, name="wgt_sb")
+        nc.sync.dma_start(wgt_sb[:], wgt)
+        bias_sb = keep.tile([P, PACK], F32, name="bias_sb")
+        nc.sync.dma_start(bias_sb[:], bias.rearrange("(p t) -> p t", t=PACK))
+        list3 = keep.tile([P, M // 16], U16, name="list3")
+        nc.sync.dma_start(list3[:], offs3)
+        wgo_sb = keep.tile([P, M], F32, name="wgo_sb")
+        nc.sync.dma_start(wgo_sb[:], wgo)
+
+        ident = keep.tile([P, P], F32, name="ident")
+        make_identity(nc, ident[:])
+        one = keep.tile([P, 1], F32, name="one")
+        nc.vector.memset(one[:], 1.0)
+        quarter_pi = keep.tile([P, 1], F32, name="quarter_pi")
+        nc.vector.tensor_scalar(quarter_pi[:], one[:], math.pi / 4, None, ALU.mult)
+
+        w4_q = keep.tile([P, 2 * N], U8, name="w4_q", align_bytes=64)
+        nc.vector.tensor_copy(
+            w4_q[:].bitcast(U16).rearrange("p (b t q) -> p b q t", t=PACK, q=P),
+            w4_raw[:].bitcast(U16).rearrange("p (b q t) -> p b q t", t=PACK, q=P))
+
+        v = [[None] * HALVES for a in range(PASSES)]
+        v_sc = keep.tile([P, S], U8, name="v_sc", align_bytes=64)
+        for a in range(PASSES):
+            for jh in range(HALVES):
+                tile = keep.tile([P, BANK], U32, name="v%d_%d" % (a, jh), align_bytes=64)
+                nc.vector.tensor_copy(tile[:], tab[a][:].indirect(list1[:, jh * BANK // 16 : (jh + 1) * BANK // 16]))
+                v[a][jh] = tile
+            if a == 0:
+                nc.vector.tensor_copy(v_sc[:], tab_sc[:].indirect(list1[:]))
+                w4_sc = stage.tile([P, N], U8, name="w4_sc", align_bytes=64, offset=0)
+                nc.vector.tensor_copy(
+                    w4_sc[:].rearrange("p (b t q) -> p b t q", t=PACK, q=P),
+                    w4_sc_raw[:].rearrange("p (b q t) -> p b t q", t=PACK, q=P))
+
+
+        def quantise(raw, name, offset):
+            grouped = stage.tile([P, PACK * H], BF16, name=name + "_grouped", align_bytes=64, offset=offset)
+            nc.vector.tensor_copy(grouped[:].rearrange("p (t q j) -> p q t j", t=PACK, j=PACK),
+                                  raw[:].rearrange("p j (q t) -> p q t j", t=PACK))
+            codes = keep.tile([P, H], U32, name=name + "_codes", align_bytes=64)
+            scales = keep.tile([P, H], U8, name=name + "_scales", align_bytes=64)
+            nc.vector.quantize_mx(codes[:].bitcast(FP8X4), scales[:], grouped[:])
+            return codes[:], scales[:]
+
+        w1_q = [quantise(w1_raw[a], "w1_%d" % a, (16 + 16 * a) * KIB) for a in range(PASSES)]
+        w3_sc = stage.tile([P, H], U8, name="w3_sc", align_bytes=64, offset=32 * KIB)
+        nc.vector.tensor_copy(w3_sc[:].rearrange("p (t q) -> p t q", t=PACK),
+                              w3_sc_raw[:].rearrange("p (q t) -> p t q", t=PACK))
+
+        w3_codes = stage.tile([P, PASSES, H], I32, name="w3_codes", align_bytes=64, offset=34 * KIB)
+        nc.vector.tensor_copy(w3_codes[:].rearrange("p a (t q) -> p a q t", t=PACK),
+                              w3_raw[:].rearrange("p a (q t) -> p a q t", t=PACK))
+        w3_q = [(w3_codes[:, a, :], w3_sc[4 * a :, :]) for a in range(PASSES)]
+
+        ref_sb = []
+        for b in range(N // K_PASS):
+            tile = stage.tile([P, PACK, M], F32, name="ref%d" % b, align_bytes=64, offset=(2 + 22 * b) * KIB)
+            nc.sync.dma_start(tile[:], ref[b * K_PASS : (b + 1) * K_PASS, :].rearrange("(p t) m -> p t m", t=PACK))
+            ref_sb.append(tile)
+
+        def product(pool, w_q, t, jh):
+            acc = pool.tile([P, BANK], F32, name="acc")
+            for a in range(PASSES):
+                codes, scales = w_q[a]
+                nc.tensor.matmul_mx(
+                    out=acc[:], lhsT=codes[:, t * P : (t + 1) * P].bitcast(FP8X4), lhsT_scale=scales[:, t * P : (t + 1) * P],
+                    rhs=v[a][jh][:].bitcast(FP8X4), rhs_scale=v_sc[4 * a :, jh * BANK : (jh + 1) * BANK],
+                    start=(a == 0), stop=(a == PASSES - 1))
+            return acc
+
+        x_rows = bf_pool.tile([P, PACK * M], BF16, name="grouped", align_bytes=64)
+        h = [keep.tile([P, S], F32, name="h%d" % t, tag="slot%d" % t) for t in range(PACK)]
+        w2_q = []
+        made = {}
+
+        def front(u):
+            t, jh = divmod(u, HALVES)
+            phase = product(psum_a, w1_q, t, jh)
+            d = product(psum_c, w3_q, t, jh)
+            s_half = work.tile([P, BANK], F32, name="w0")
+            nc.scalar.activation(s_half[:], phase[:], ACT.Sin, scale=0.5)
+            if u < PASSES:
+                one_minus_cos = stage.tile([P, BANK], F32, name="omc%d" % u, align_bytes=64, offset=(10 + 10 * u) * KIB)
+            else:
+                one_minus_cos = work.tile([P, BANK], F32, name="w2")
+            nc.scalar.activation(one_minus_cos[:], s_half[:], ACT.Square, scale=math.sqrt(2.0))
+            s_shift = work.tile([P, BANK], F32, name="w1")
+            nc.scalar.activation(s_shift[:], phase[:], ACT.Sin, scale=0.5, bias=quarter_pi[:])
+            one_plus_sin = cos_pool.tile([P, BANK], F32, name="one_plus_sin")
+            nc.scalar.activation(one_plus_sin[:], s_shift[:], ACT.Square, scale=math.sqrt(2.0))
+            neg_cos_d = cos_pool.tile([P, BANK], F32, name="neg_cos_d")
+            nc.vector.scalar_tensor_tensor(neg_cos_d[:], one_minus_cos[:], 1.0, d[:], ALU.subtract, ALU.mult)
+            made[u] = (one_plus_sin, neg_cos_d)
+            if u < PASSES:
+                w2_q.append(quantise(w2_raw[u], "w2_%d" % u, (10 + 10 * u) * KIB))
+
+        def back(u):
+            t, jh = divmod(u, HALVES)
+            one_plus_sin, neg_cos_d = made[u]
+            b = product(psum_b, w2_q, t, jh)
+            sin_b = work.tile([P, BANK], F32, name="w4")
+            nc.vector.scalar_tensor_tensor(sin_b[:], one_plus_sin[:], 1.0, b[:], ALU.subtract, ALU.mult)
+            nc.vector.scalar_tensor_tensor(h[t][:, jh * BANK : (jh + 1) * BANK], neg_cos_d[:], -1.0, sin_b[:],
+                                           ALU.mult, ALU.max)
+            if jh == HALVES - 1:
+                picked = work.tile([P, M], F32, name="w5")
+                nc.vector.tensor_tensor(picked[:], h[t][:].indirect(list2[:]), wgt_sb[:], ALU.mult)
+                nc.scalar.activation(x_rows[:, t * M : (t + 1) * M], picked[:], ACT.Identity, bias=bias_sb[:, t : t + 1])
+
+        for u in range(UNITS + AHEAD):
+            if u < UNITS:
+                front(u)
+            if u >= AHEAD:
+                back(u - AHEAD)
+
+        x_grouped = bf_pool.tile([P, PACK * M], BF16, name="grouped", align_bytes=64)
+        nc.vector.tensor_copy(x_grouped[:].rearrange("p (c i t) -> p c t i", i=4, t=PACK),
+                              x_rows[:].rearrange("p (t c i) -> p c t i", i=4, t=PACK))
+        x_codes = keep.tile([P, M], U32, name="x_codes", align_bytes=64)
+        x_scales = keep.tile([P, M], U8, name="x_scales", align_bytes=64)
+        nc.vector.quantize_mx(x_codes[:].bitcast(FP8X4), x_scales[:], x_grouped[:])
+
+        out_rows = out.rearrange("(b p t) c -> b t p c", p=P, t=PACK)
+        for i in range(OUT_TILES):
+            b, t = divmod(i, PACK)
+            ref_i = ref_sb[b][:, t, :]
+            if t == 0:
+                page = stage.tile([P, T2], F32, name="page%d" % i, align_bytes=64, offset=20 * KIB)
+            else:
+                page = keep.tile([P, T2], F32, name="page%d" % i, tag="slot%d" % (t - 1))
+            nc.gpsimd.memset(page[:], 0.0)
+            acc = psum_b.tile([P, M], F32, name="acc")
+            nc.tensor.matmul_mx(
+                out=acc[:], lhsT=w4_q[:, 2 * i * P : 2 * (i + 1) * P].bitcast(FP4X4), lhsT_scale=w4_sc[:, i * P : (i + 1) * P],
+                rhs=x_codes[:].bitcast(FP8X4), rhs_scale=x_scales[:], start=True, stop=True)
+            y = work.tile([P, M], F32, name="w3")
+            if i < DIRECT_TILES:
+                e = work.tile([P, M], F32, name="w0")
+                nc.vector.tensor_tensor(e[:], acc[:], ref_i, ALU.subtract)
+                e_abs = work.tile([P, M], F32, name="w1")
+                if i == 0:
+                    nc.vector.scalar_tensor_tensor(e_abs[:], e[:], -1.0, e[:], ALU.mult, ALU.max)
+                else:
+                    nc.scalar.activation(e_abs[:], e[:], ACT.Abs)
+                nc.scalar.activation(y[:], e_abs[:], ACT.Sqrt, bias=one[:])
+            else:
+                neg = work.tile([P, M], F32, name="w0")
+                nc.scalar.activation(neg[:], acc[:], ACT.Copy, scale=-1.0)
+                e_t = psum_a.tile([P, M], F32, name="acc")
+                blocks = [slice(c * P, (c + 1) * P) for c in range(M // P)]
+                for c, cols in enumerate(blocks):
+                    nc.tensor.matmul(e_t[:, cols], ref_i[:, cols], ident[:], start=(c == 0), stop=False, is_transpose=True)
+                for c, cols in enumerate(blocks):
+                    nc.tensor.matmul(e_t[:, cols], neg[:, cols], ident[:], start=False, stop=(c == len(blocks) - 1),
+                                     is_transpose=True)
+                abs_t = work.tile([P, M], F32, name="w1")
+                nc.scalar.activation(abs_t[:], e_t[:], ACT.Abs)
+                e_abs = psum_c.tile([P, M], F32, name="acc")
+                for cols in blocks:
+                    nc.tensor.transpose(e_abs[:, cols], abs_t[:, cols], ident[:])
+                nc.scalar.activation(y[:], e_abs[:], ACT.Sqrt, bias=one[:])
+            nc.vector.tensor_tensor(page[:].indirect(list3[:]), y[:], wgo_sb[:], ALU.mult)
+            nc.sync.dma_start(out_rows[b, t], page[:])

@@ -25,9 +25,9 @@ PASSES = K // K_PASS
 BANK = 512
 HALVES = S // BANK
 OUT_TILES = N // P
-DIRECT_TILES = 2
 KIB = 1024
 AHEAD = 2
+MH = M // 2
 UNITS = PACK * HALVES
 
 
@@ -39,7 +39,6 @@ def tile_list_spirometry_obstruction_slots_kernel(
     with ExitStack() as ctx:
         keep = ctx.enter_context(tc.tile_pool(name="keep", bufs=1))
         raw_pool = ctx.enter_context(tc.tile_pool(name="raw", bufs=4))
-        bf_pool = ctx.enter_context(tc.tile_pool(name="bf", bufs=2))
         stage = ctx.enter_context(tc.tile_pool(name="stage", bufs=1))
         work = ctx.enter_context(tc.tile_pool(name="work", bufs=3))
         cos_pool = ctx.enter_context(tc.tile_pool(name="cosd", bufs=4))
@@ -55,33 +54,33 @@ def tile_list_spirometry_obstruction_slots_kernel(
 
         list1 = keep.tile([P, S // 16], U16, name="list1")
         nc.sync.dma_start(list1[:], offs)
-        w4_raw = keep.tile([P, 2 * N], U8, name="w4_raw", align_bytes=64)
-        nc.sync.dma_start(w4_raw[:].bitcast(I32), w4_words[0].bitcast(I32))
-        tab = []
-        for a in range(PASSES):
-            tile = stage.tile([P, T], U32, name="tab%d" % a, align_bytes=64, offset=16 * KIB * a)
-            nc.sync.dma_start(tile[:].bitcast(I32), tab_words[a].rearrange("p t i -> p (t i)").bitcast(I32))
-            tab.append(tile)
+        tab = [stage.tile([P, T], U32, name="tab%d" % a, align_bytes=64, offset=16 * KIB * a) for a in range(PASSES)]
+
+        def load_tab(a):
+            nc.sync.dma_start(tab[a][:].bitcast(I32), tab_words[a].rearrange("p t i -> p (t i)").bitcast(I32))
 
         def load_raw(w, a):
             tile = raw_pool.tile([P, PACK, H], F32, name="raw")
             nc.sync.dma_start(tile[:], w[a * K_PASS : (a + 1) * K_PASS, :].rearrange("(p j) c -> p j c", j=PACK))
             return tile
 
-        w1_raw = [load_raw(w1, a) for a in range(PASSES)]
+        def load_planes(queue, plane, scales):
+            for q in range(4):
+                queue.dma_start(plane[32 * q : 32 * q + 4 * scales.shape[0], :].bitcast(I32),
+                                scales[:, 4 * q : 4 * q + 4, :].bitcast(I32))
+
+        load_tab(0)
+        load_planes(nc.gpsimd, tab_sc, tab_scales)
+        load_planes(nc.sync, w4_sc_raw, w4_scales)
+        w4_raw = keep.tile([P, 2 * N], U8, name="w4_raw", align_bytes=64)
+        nc.sync.dma_start(w4_raw[:].bitcast(I32), w4_words[0].bitcast(I32))
+        w1_raw = [load_raw(w1, 0)]
+        load_planes(nc.sync, w3_sc_raw, w3_scales)
+        w1_raw.append(load_raw(w1, 1))
+        load_tab(1)
         w3_raw = keep.tile([P, PASSES, H], I32, name="w3_raw", align_bytes=64)
         nc.sync.dma_start(w3_raw[:], w3_words.rearrange("a p c i -> p a (c i)").bitcast(I32))
         w2_raw = [load_raw(w2, a) for a in range(PASSES)]
-
-        for q in range(4):
-            nc.gpsimd.dma_start(tab_sc[32 * q : 32 * q + 4 * PASSES, :].bitcast(I32),
-                                tab_scales[:, 4 * q : 4 * q + 4, :].bitcast(I32))
-        for q in range(4):
-            nc.gpsimd.dma_start(w4_sc_raw[32 * q : 32 * q + 4, :].bitcast(I32),
-                                w4_scales[0, 4 * q : 4 * q + 4, :].bitcast(I32))
-        for q in range(4):
-            nc.gpsimd.dma_start(w3_sc_raw[32 * q : 32 * q + 4 * PASSES, :].bitcast(I32),
-                                w3_scales[:, 4 * q : 4 * q + 4, :].bitcast(I32))
 
         list2 = keep.tile([P, M // 16], U16, name="list2")
         nc.sync.dma_start(list2[:], offs2)
@@ -101,41 +100,52 @@ def tile_list_spirometry_obstruction_slots_kernel(
         quarter_pi = keep.tile([P, 1], F32, name="quarter_pi")
         nc.vector.tensor_scalar(quarter_pi[:], one[:], math.pi / 4, None, ALU.mult)
 
+        pages = []
+        for i in range(OUT_TILES):
+            page = keep.tile([P, T2], F32, name="page%d" % i)
+            nc.vector.memset(page[:], 0.0)
+            pages.append(page)
+
         w4_q = keep.tile([P, 2 * N], U8, name="w4_q", align_bytes=64)
         nc.vector.tensor_copy(
             w4_q[:].bitcast(U16).rearrange("p (b t q) -> p b q t", t=PACK, q=P),
             w4_raw[:].bitcast(U16).rearrange("p (b q t) -> p b q t", t=PACK, q=P))
 
+
         v = [[None] * HALVES for a in range(PASSES)]
-        v_sc = keep.tile([P, S], U8, name="v_sc", align_bytes=64)
-        for a in range(PASSES):
+
+        def gather_words(a):
             for jh in range(HALVES):
                 tile = keep.tile([P, BANK], U32, name="v%d_%d" % (a, jh), align_bytes=64)
                 nc.vector.tensor_copy(tile[:], tab[a][:].indirect(list1[:, jh * BANK // 16 : (jh + 1) * BANK // 16]))
                 v[a][jh] = tile
-            if a == 0:
-                nc.vector.tensor_copy(v_sc[:], tab_sc[:].indirect(list1[:]))
-                w4_sc = stage.tile([P, N], U8, name="w4_sc", align_bytes=64, offset=0)
-                nc.vector.tensor_copy(
-                    w4_sc[:].rearrange("p (b t q) -> p b t q", t=PACK, q=P),
-                    w4_sc_raw[:].rearrange("p (b q t) -> p b t q", t=PACK, q=P))
 
-
-        def quantise(raw, name, offset):
+        def quantise(raw, name, offset, scalar_share):
             grouped = stage.tile([P, PACK * H], BF16, name=name + "_grouped", align_bytes=64, offset=offset)
-            nc.vector.tensor_copy(grouped[:].rearrange("p (t q j) -> p q t j", t=PACK, j=PACK),
-                                  raw[:].rearrange("p j (q t) -> p q t j", t=PACK))
+            dealt = grouped[:].rearrange("p (t q j) -> p q j t", t=PACK, j=PACK)
+            rows = raw[:].rearrange("p j (q t) -> p q j t", t=PACK)
+            if scalar_share > 0:
+                nc.scalar.copy(dealt[:, :scalar_share], rows[:, :scalar_share])
+            if scalar_share < P:
+                nc.vector.tensor_copy(dealt[:, scalar_share:], rows[:, scalar_share:])
             codes = keep.tile([P, H], U32, name=name + "_codes", align_bytes=64)
             scales = keep.tile([P, H], U8, name=name + "_scales", align_bytes=64)
             nc.vector.quantize_mx(codes[:].bitcast(FP8X4), scales[:], grouped[:])
             return codes[:], scales[:]
 
-        w1_q = [quantise(w1_raw[a], "w1_%d" % a, (16 + 16 * a) * KIB) for a in range(PASSES)]
-        w3_sc = stage.tile([P, H], U8, name="w3_sc", align_bytes=64, offset=32 * KIB)
-        nc.vector.tensor_copy(w3_sc[:].rearrange("p (t q) -> p t q", t=PACK),
-                              w3_sc_raw[:].rearrange("p (q t) -> p t q", t=PACK))
-
-        w3_codes = stage.tile([P, PASSES, H], I32, name="w3_codes", align_bytes=64, offset=34 * KIB)
+        gather_words(0)
+        v_sc = keep.tile([P, S], U8, name="v_sc", align_bytes=64)
+        nc.vector.tensor_copy(v_sc[:], tab_sc[:].indirect(list1[:]))
+        w4_sc = stage.tile([P, N], U8, name="w4_sc", align_bytes=64, offset=KIB)
+        nc.vector.tensor_copy(w4_sc[:].rearrange("p (b t q) -> p b q t", t=PACK, q=P),
+                              w4_sc_raw[:].rearrange("p (b q t) -> p b q t", t=PACK, q=P))
+        w3_sc = stage.tile([P, H], U8, name="w3_sc", align_bytes=64, offset=0)
+        nc.vector.tensor_copy(w3_sc[:].rearrange("p (t q) -> p q t", t=PACK),
+                              w3_sc_raw[:].rearrange("p (q t) -> p q t", t=PACK))
+        w1_q = [quantise(w1_raw[0], "w1_0", 36 * KIB, P),
+                quantise(w1_raw[1], "w1_1", 32 * KIB, P // 2)]
+        gather_words(1)
+        w3_codes = stage.tile([P, PASSES, H], I32, name="w3_codes", align_bytes=64, offset=16 * KIB)
         nc.vector.tensor_copy(w3_codes[:].rearrange("p a (t q) -> p a q t", t=PACK),
                               w3_raw[:].rearrange("p a (q t) -> p a q t", t=PACK))
         w3_q = [(w3_codes[:, a, :], w3_sc[4 * a :, :]) for a in range(PASSES)]
@@ -156,8 +166,8 @@ def tile_list_spirometry_obstruction_slots_kernel(
                     start=(a == 0), stop=(a == PASSES - 1))
             return acc
 
-        x_rows = bf_pool.tile([P, PACK * M], BF16, name="grouped", align_bytes=64)
-        h = [keep.tile([P, S], F32, name="h%d" % t, tag="slot%d" % t) for t in range(PACK)]
+        x_rows = [keep.tile([P, PACK * MH], BF16, name="x_rows%d" % mh, align_bytes=64) for mh in range(2)]
+        h = [keep.tile([P, S], F32, name="h%d" % t) for t in range(PACK)]
         w2_q = []
         made = {}
 
@@ -176,24 +186,34 @@ def tile_list_spirometry_obstruction_slots_kernel(
             nc.scalar.activation(s_shift[:], phase[:], ACT.Sin, scale=0.5, bias=quarter_pi[:])
             one_plus_sin = cos_pool.tile([P, BANK], F32, name="one_plus_sin")
             nc.scalar.activation(one_plus_sin[:], s_shift[:], ACT.Square, scale=math.sqrt(2.0))
-            neg_cos_d = cos_pool.tile([P, BANK], F32, name="neg_cos_d")
+            if 1 <= u <= PASSES:
+                neg_cos_d = stage.tile([P, BANK], F32, name="ncd%d" % u, align_bytes=64, offset=10 * u * KIB)
+            else:
+                neg_cos_d = cos_pool.tile([P, BANK], F32, name="neg_cos_d")
             nc.vector.scalar_tensor_tensor(neg_cos_d[:], one_minus_cos[:], 1.0, d[:], ALU.subtract, ALU.mult)
             made[u] = (one_plus_sin, neg_cos_d)
             if u < PASSES:
-                w2_q.append(quantise(w2_raw[u], "w2_%d" % u, (10 + 10 * u) * KIB))
+                w2_q.append(quantise(w2_raw[u], "w2_%d" % u, (10 + 10 * u) * KIB, 0))
+
+        def pick(t, mh, picked):
+            nc.vector.tensor_tensor(picked[:], h[t][:].indirect(list2[:, mh * MH // 16 : (mh + 1) * MH // 16]),
+                                    wgt_sb[:, mh * MH : (mh + 1) * MH], ALU.mult)
+            nc.scalar.activation(x_rows[mh][:, t * MH : (t + 1) * MH], picked[:], ACT.Identity, bias=bias_sb[:, t : t + 1])
 
         def back(u):
             t, jh = divmod(u, HALVES)
             one_plus_sin, neg_cos_d = made[u]
             b = product(psum_b, w2_q, t, jh)
-            sin_b = work.tile([P, BANK], F32, name="w4")
+            if u == UNITS - 1:
+                sin_b = stage.tile([P, BANK], F32, name="sin_b_last", align_bytes=64, offset=36 * KIB)
+            else:
+                sin_b = work.tile([P, BANK], F32, name="w4")
             nc.vector.scalar_tensor_tensor(sin_b[:], one_plus_sin[:], 1.0, b[:], ALU.subtract, ALU.mult)
             nc.vector.scalar_tensor_tensor(h[t][:, jh * BANK : (jh + 1) * BANK], neg_cos_d[:], -1.0, sin_b[:],
                                            ALU.mult, ALU.max)
             if jh == HALVES - 1:
-                picked = work.tile([P, M], F32, name="w5")
-                nc.vector.tensor_tensor(picked[:], h[t][:].indirect(list2[:]), wgt_sb[:], ALU.mult)
-                nc.scalar.activation(x_rows[:, t * M : (t + 1) * M], picked[:], ACT.Identity, bias=bias_sb[:, t : t + 1])
+                picked = work.tile([P, MH], F32, name="w5")
+                pick(t, 0, picked)
 
         for u in range(UNITS + AHEAD):
             if u < UNITS:
@@ -201,51 +221,50 @@ def tile_list_spirometry_obstruction_slots_kernel(
             if u >= AHEAD:
                 back(u - AHEAD)
 
-        x_grouped = bf_pool.tile([P, PACK * M], BF16, name="grouped", align_bytes=64)
-        nc.vector.tensor_copy(x_grouped[:].rearrange("p (c i t) -> p c t i", i=4, t=PACK),
-                              x_rows[:].rearrange("p (t c i) -> p c t i", i=4, t=PACK))
-        x_codes = keep.tile([P, M], U32, name="x_codes", align_bytes=64)
-        x_scales = keep.tile([P, M], U8, name="x_scales", align_bytes=64)
-        nc.vector.quantize_mx(x_codes[:].bitcast(FP8X4), x_scales[:], x_grouped[:])
+        def quantise_x(mh, offset):
+            grouped = stage.tile([P, PACK * MH], BF16, name="x_grouped%d" % mh, align_bytes=64, offset=offset)
+            nc.vector.tensor_copy(grouped[:].rearrange("p (c i t) -> p c t i", i=4, t=PACK),
+                                  x_rows[mh][:].rearrange("p (t c i) -> p c t i", i=4, t=PACK))
+            codes = keep.tile([P, MH], U32, name="x_codes%d" % mh, align_bytes=64)
+            scales = keep.tile([P, MH], U8, name="x_scales%d" % mh, align_bytes=64)
+            nc.vector.quantize_mx(codes[:].bitcast(FP8X4), scales[:], grouped[:])
+            return codes, scales
+
+        x_q = [quantise_x(0, 33 * KIB)]
+        for t in range(PACK):
+            offset = 36 * KIB if t == 0 else (32 + t) * KIB - KIB // 2
+            picked = stage.tile([P, MH], F32, name="picked%d" % t, align_bytes=64, offset=offset)
+            pick(t, 1, picked)
+        x_q.append(quantise_x(1, 38 * KIB))
 
         out_rows = out.rearrange("(b p t) c -> b t p c", p=P, t=PACK)
-        for i in range(OUT_TILES):
-            b, t = divmod(i, PACK)
-            ref_i = ref_sb[b][:, t, :]
-            if t == 0:
-                page = stage.tile([P, T2], F32, name="page%d" % i, align_bytes=64, offset=20 * KIB)
-            else:
-                page = keep.tile([P, T2], F32, name="page%d" % i, tag="slot%d" % (t - 1))
-            nc.gpsimd.memset(page[:], 0.0)
-            acc = psum_b.tile([P, M], F32, name="acc")
-            nc.tensor.matmul_mx(
-                out=acc[:], lhsT=w4_q[:, 2 * i * P : 2 * (i + 1) * P].bitcast(FP4X4), lhsT_scale=w4_sc[:, i * P : (i + 1) * P],
-                rhs=x_codes[:].bitcast(FP8X4), rhs_scale=x_scales[:], start=True, stop=True)
-            y = work.tile([P, M], F32, name="w3")
-            if i < DIRECT_TILES:
-                e = work.tile([P, M], F32, name="w0")
-                nc.vector.tensor_tensor(e[:], acc[:], ref_i, ALU.subtract)
-                e_abs = work.tile([P, M], F32, name="w1")
-                if i == 0:
-                    nc.vector.scalar_tensor_tensor(e_abs[:], e[:], -1.0, e[:], ALU.mult, ALU.max)
-                else:
-                    nc.scalar.activation(e_abs[:], e[:], ACT.Abs)
-                nc.scalar.activation(y[:], e_abs[:], ACT.Sqrt, bias=one[:])
-            else:
-                neg = work.tile([P, M], F32, name="w0")
+        blocks = [slice(c * P, (c + 1) * P) for c in range(MH // P)]
+        for mh in range(2):
+            x_codes, x_scales = x_q[mh]
+            for i in range(OUT_TILES):
+                b, t = divmod(i, PACK)
+                ref_i = ref_sb[b][:, t, mh * MH : (mh + 1) * MH]
+                acc = psum_b.tile([P, MH], F32, name="acc")
+                nc.tensor.matmul_mx(
+                    out=acc[:], lhsT=w4_q[:, 2 * i * P : 2 * (i + 1) * P].bitcast(FP4X4),
+                    lhsT_scale=w4_sc[:, i * P : (i + 1) * P],
+                    rhs=x_codes[:].bitcast(FP8X4), rhs_scale=x_scales[:], start=True, stop=True)
+                neg = work.tile([P, MH], F32, name="w0")
                 nc.scalar.activation(neg[:], acc[:], ACT.Copy, scale=-1.0)
-                e_t = psum_a.tile([P, M], F32, name="acc")
-                blocks = [slice(c * P, (c + 1) * P) for c in range(M // P)]
+                e_t = psum_a.tile([P, MH], F32, name="acc")
                 for c, cols in enumerate(blocks):
                     nc.tensor.matmul(e_t[:, cols], ref_i[:, cols], ident[:], start=(c == 0), stop=False, is_transpose=True)
                 for c, cols in enumerate(blocks):
                     nc.tensor.matmul(e_t[:, cols], neg[:, cols], ident[:], start=False, stop=(c == len(blocks) - 1),
                                      is_transpose=True)
-                abs_t = work.tile([P, M], F32, name="w1")
+                abs_t = work.tile([P, MH], F32, name="w1")
                 nc.scalar.activation(abs_t[:], e_t[:], ACT.Abs)
-                e_abs = psum_c.tile([P, M], F32, name="acc")
+                e_abs = psum_c.tile([P, MH], F32, name="acc")
                 for cols in blocks:
                     nc.tensor.transpose(e_abs[:, cols], abs_t[:, cols], ident[:])
+                y = work.tile([P, MH], F32, name="w3")
                 nc.scalar.activation(y[:], e_abs[:], ACT.Sqrt, bias=one[:])
-            nc.vector.tensor_tensor(page[:].indirect(list3[:]), y[:], wgo_sb[:], ALU.mult)
-            nc.sync.dma_start(out_rows[b, t], page[:])
+                nc.vector.tensor_tensor(pages[i][:].indirect(list3[:, mh * MH // 16 : (mh + 1) * MH // 16]), y[:],
+                                        wgo_sb[:, mh * MH : (mh + 1) * MH], ALU.mult)
+                if mh == 1:
+                    nc.sync.dma_start(out_rows[b, t], pages[i][:])

@@ -27,6 +27,9 @@ HALVES = S // BANK
 OUT_TILES = N // P
 KIB = 1024
 AHEAD = 2
+W2_SCALAR_SHARE = 48
+PAGE_BUFS = 4
+SPLIT_TILES = 3
 MH = M // 2
 UNITS = PACK * HALVES
 
@@ -38,7 +41,7 @@ def tile_list_spirometry_obstruction_slots_kernel(
     nc = tc.nc
     with ExitStack() as ctx:
         keep = ctx.enter_context(tc.tile_pool(name="keep", bufs=1))
-        raw_pool = ctx.enter_context(tc.tile_pool(name="raw", bufs=4))
+        page_pool = ctx.enter_context(tc.tile_pool(name="pages", bufs=PAGE_BUFS))
         stage = ctx.enter_context(tc.tile_pool(name="stage", bufs=1))
         work = ctx.enter_context(tc.tile_pool(name="work", bufs=3))
         cos_pool = ctx.enter_context(tc.tile_pool(name="cosd", bufs=4))
@@ -59,28 +62,27 @@ def tile_list_spirometry_obstruction_slots_kernel(
         def load_tab(a):
             nc.sync.dma_start(tab[a][:].bitcast(I32), tab_words[a].rearrange("p t i -> p (t i)").bitcast(I32))
 
-        def load_raw(w, a):
-            tile = raw_pool.tile([P, PACK, H], F32, name="raw")
+        def load_raw(w, a, offset):
+            tile = stage.tile([P, PACK, H], F32, name="raw%d" % (offset // KIB), align_bytes=64, offset=offset)
             nc.sync.dma_start(tile[:], w[a * K_PASS : (a + 1) * K_PASS, :].rearrange("(p j) c -> p j c", j=PACK))
             return tile
 
-        def load_planes(queue, plane, scales):
+        def load_planes(plane, scales):
             for q in range(4):
-                queue.dma_start(plane[32 * q : 32 * q + 4 * scales.shape[0], :].bitcast(I32),
+                nc.sync.dma_start(plane[32 * q : 32 * q + 4 * scales.shape[0], :].bitcast(I32),
                                 scales[:, 4 * q : 4 * q + 4, :].bitcast(I32))
 
         load_tab(0)
-        load_planes(nc.gpsimd, tab_sc, tab_scales)
-        load_planes(nc.sync, w4_sc_raw, w4_scales)
+        load_planes(tab_sc, tab_scales)
+        w1_raw = [load_raw(w1, a, (40 + 8 * a) * KIB) for a in range(PASSES)]
         w4_raw = keep.tile([P, 2 * N], U8, name="w4_raw", align_bytes=64)
         nc.sync.dma_start(w4_raw[:].bitcast(I32), w4_words[0].bitcast(I32))
-        w1_raw = [load_raw(w1, 0)]
-        load_planes(nc.sync, w3_sc_raw, w3_scales)
-        w1_raw.append(load_raw(w1, 1))
+        load_planes(w4_sc_raw, w4_scales)
         load_tab(1)
+        load_planes(w3_sc_raw, w3_scales)
         w3_raw = keep.tile([P, PASSES, H], I32, name="w3_raw", align_bytes=64)
         nc.sync.dma_start(w3_raw[:], w3_words.rearrange("a p c i -> p a (c i)").bitcast(I32))
-        w2_raw = [load_raw(w2, a) for a in range(PASSES)]
+        w2_raw = [load_raw(w2, a, (56 + 8 * a) * KIB) for a in range(PASSES)]
 
         list2 = keep.tile([P, M // 16], U16, name="list2")
         nc.sync.dma_start(list2[:], offs2)
@@ -101,15 +103,15 @@ def tile_list_spirometry_obstruction_slots_kernel(
         nc.vector.tensor_scalar(quarter_pi[:], one[:], math.pi / 4, None, ALU.mult)
 
         pages = []
-        for i in range(OUT_TILES):
-            page = keep.tile([P, T2], F32, name="page%d" % i)
+        for i in range(PAGE_BUFS):
+            page = page_pool.tile([P, T2], F32, name="page")
             nc.vector.memset(page[:], 0.0)
             pages.append(page)
 
         w4_q = keep.tile([P, 2 * N], U8, name="w4_q", align_bytes=64)
         nc.vector.tensor_copy(
-            w4_q[:].bitcast(U16).rearrange("p (b t q) -> p b q t", t=PACK, q=P),
-            w4_raw[:].bitcast(U16).rearrange("p (b q t) -> p b q t", t=PACK, q=P))
+            w4_q[:].bitcast(U16).rearrange("p (b t q) -> p b t q", t=PACK, q=P),
+            w4_raw[:].bitcast(U16).rearrange("p (b q t) -> p b t q", t=PACK, q=P))
 
 
         v = [[None] * HALVES for a in range(PASSES)]
@@ -122,8 +124,8 @@ def tile_list_spirometry_obstruction_slots_kernel(
 
         def quantise(raw, name, offset, scalar_share):
             grouped = stage.tile([P, PACK * H], BF16, name=name + "_grouped", align_bytes=64, offset=offset)
-            dealt = grouped[:].rearrange("p (t q j) -> p q j t", t=PACK, j=PACK)
-            rows = raw[:].rearrange("p j (q t) -> p q j t", t=PACK)
+            dealt = grouped[:].rearrange("p (t q j) -> p q t j", t=PACK, j=PACK)
+            rows = raw[:].rearrange("p j (q t) -> p q t j", t=PACK)
             if scalar_share > 0:
                 nc.scalar.copy(dealt[:, :scalar_share], rows[:, :scalar_share])
             if scalar_share < P:
@@ -137,14 +139,14 @@ def tile_list_spirometry_obstruction_slots_kernel(
         v_sc = keep.tile([P, S], U8, name="v_sc", align_bytes=64)
         nc.vector.tensor_copy(v_sc[:], tab_sc[:].indirect(list1[:]))
         w4_sc = stage.tile([P, N], U8, name="w4_sc", align_bytes=64, offset=KIB)
-        nc.vector.tensor_copy(w4_sc[:].rearrange("p (b t q) -> p b q t", t=PACK, q=P),
-                              w4_sc_raw[:].rearrange("p (b q t) -> p b q t", t=PACK, q=P))
-        w3_sc = stage.tile([P, H], U8, name="w3_sc", align_bytes=64, offset=0)
-        nc.vector.tensor_copy(w3_sc[:].rearrange("p (t q) -> p q t", t=PACK),
-                              w3_sc_raw[:].rearrange("p (q t) -> p q t", t=PACK))
+        nc.vector.tensor_copy(w4_sc[:].rearrange("p (b t q) -> p b t q", t=PACK, q=P),
+                              w4_sc_raw[:].rearrange("p (b q t) -> p b t q", t=PACK, q=P))
         w1_q = [quantise(w1_raw[0], "w1_0", 36 * KIB, P),
                 quantise(w1_raw[1], "w1_1", 32 * KIB, P // 2)]
         gather_words(1)
+        w3_sc = stage.tile([P, H], U8, name="w3_sc", align_bytes=64, offset=0)
+        nc.vector.tensor_copy(w3_sc[:].rearrange("p (t q) -> p t q", t=PACK),
+                              w3_sc_raw[:].rearrange("p (q t) -> p t q", t=PACK))
         w3_codes = stage.tile([P, PASSES, H], I32, name="w3_codes", align_bytes=64, offset=16 * KIB)
         nc.vector.tensor_copy(w3_codes[:].rearrange("p a (t q) -> p a q t", t=PACK),
                               w3_raw[:].rearrange("p a (q t) -> p a q t", t=PACK))
@@ -168,32 +170,30 @@ def tile_list_spirometry_obstruction_slots_kernel(
 
         x_rows = [keep.tile([P, PACK * MH], BF16, name="x_rows%d" % mh, align_bytes=64) for mh in range(2)]
         h = [keep.tile([P, S], F32, name="h%d" % t) for t in range(PACK)]
-        w2_q = []
+        w2_q = [quantise(w2_raw[a], "w2_%d" % a, (10 + 10 * a) * KIB, W2_SCALAR_SHARE) for a in range(PASSES)]
         made = {}
 
         def front(u):
             t, jh = divmod(u, HALVES)
             phase = product(psum_a, w1_q, t, jh)
             d = product(psum_c, w3_q, t, jh)
-            s_half = work.tile([P, BANK], F32, name="w0")
+            held = [125 * KIB // 2 + 2 * KIB * slot for slot in range(5)]
+            s_half = stage.tile([P, BANK], F32, name="s_half%d" % u, align_bytes=64,
+                                offset=(40 * KIB, 58 * KIB)[u] if u < 2 else held[u % 2])
             nc.scalar.activation(s_half[:], phase[:], ACT.Sin, scale=0.5)
-            if u < PASSES:
-                one_minus_cos = stage.tile([P, BANK], F32, name="omc%d" % u, align_bytes=64, offset=(10 + 10 * u) * KIB)
+            if u == 1:
+                one_minus_cos = stage.tile([P, BANK], F32, name="omc%d" % u, align_bytes=64, offset=held[4])
             else:
                 one_minus_cos = work.tile([P, BANK], F32, name="w2")
             nc.scalar.activation(one_minus_cos[:], s_half[:], ACT.Square, scale=math.sqrt(2.0))
-            s_shift = work.tile([P, BANK], F32, name="w1")
+            s_shift = stage.tile([P, BANK], F32, name="s_shift%d" % u, align_bytes=64,
+                                 offset=42 * KIB if u == 0 else held[2 + u % 2])
             nc.scalar.activation(s_shift[:], phase[:], ACT.Sin, scale=0.5, bias=quarter_pi[:])
             one_plus_sin = cos_pool.tile([P, BANK], F32, name="one_plus_sin")
             nc.scalar.activation(one_plus_sin[:], s_shift[:], ACT.Square, scale=math.sqrt(2.0))
-            if 1 <= u <= PASSES:
-                neg_cos_d = stage.tile([P, BANK], F32, name="ncd%d" % u, align_bytes=64, offset=10 * u * KIB)
-            else:
-                neg_cos_d = cos_pool.tile([P, BANK], F32, name="neg_cos_d")
+            neg_cos_d = stage.tile([P, BANK], F32, name="ncd%d" % u, align_bytes=64, offset=(56, 10, 20)[u % 3] * KIB)
             nc.vector.scalar_tensor_tensor(neg_cos_d[:], one_minus_cos[:], 1.0, d[:], ALU.subtract, ALU.mult)
             made[u] = (one_plus_sin, neg_cos_d)
-            if u < PASSES:
-                w2_q.append(quantise(w2_raw[u], "w2_%d" % u, (10 + 10 * u) * KIB, 0))
 
         def pick(t, mh, picked):
             nc.vector.tensor_tensor(picked[:], h[t][:].indirect(list2[:, mh * MH // 16 : (mh + 1) * MH // 16]),
@@ -221,50 +221,60 @@ def tile_list_spirometry_obstruction_slots_kernel(
             if u >= AHEAD:
                 back(u - AHEAD)
 
+        x_codes = keep.tile([P, M], U32, name="x_codes", align_bytes=64)
+        x_scales = keep.tile([P, M], U8, name="x_scales", align_bytes=64)
+
         def quantise_x(mh, offset):
             grouped = stage.tile([P, PACK * MH], BF16, name="x_grouped%d" % mh, align_bytes=64, offset=offset)
             nc.vector.tensor_copy(grouped[:].rearrange("p (c i t) -> p c t i", i=4, t=PACK),
                                   x_rows[mh][:].rearrange("p (t c i) -> p c t i", i=4, t=PACK))
-            codes = keep.tile([P, MH], U32, name="x_codes%d" % mh, align_bytes=64)
-            scales = keep.tile([P, MH], U8, name="x_scales%d" % mh, align_bytes=64)
-            nc.vector.quantize_mx(codes[:].bitcast(FP8X4), scales[:], grouped[:])
-            return codes, scales
+            cols = slice(mh * MH, (mh + 1) * MH)
+            nc.vector.quantize_mx(x_codes[:, cols].bitcast(FP8X4), x_scales[:, cols], grouped[:])
 
-        x_q = [quantise_x(0, 33 * KIB)]
+        quantise_x(0, 33 * KIB)
         for t in range(PACK):
             offset = 36 * KIB if t == 0 else (32 + t) * KIB - KIB // 2
             picked = stage.tile([P, MH], F32, name="picked%d" % t, align_bytes=64, offset=offset)
             pick(t, 1, picked)
-        x_q.append(quantise_x(1, 38 * KIB))
+        quantise_x(1, 38 * KIB)
 
         out_rows = out.rearrange("(b p t) c -> b t p c", p=P, t=PACK)
-        blocks = [slice(c * P, (c + 1) * P) for c in range(MH // P)]
+
+        def score(i, m0, m1):
+            b, t = divmod(i, PACK)
+            width = m1 - m0
+            blocks = [slice(c * P, (c + 1) * P) for c in range(width // P)]
+            ref_i = ref_sb[b][:, t, m0:m1]
+            acc = psum_b.tile([P, width], F32, name="acc")
+            nc.tensor.matmul_mx(
+                out=acc[:], lhsT=w4_q[:, 2 * i * P : 2 * (i + 1) * P].bitcast(FP4X4),
+                lhsT_scale=w4_sc[:, i * P : (i + 1) * P],
+                rhs=x_codes[:, m0:m1].bitcast(FP8X4), rhs_scale=x_scales[:, m0:m1], start=True, stop=True)
+            neg = work.tile([P, width], F32, name="w0")
+            nc.scalar.activation(neg[:], acc[:], ACT.Copy, scale=-1.0)
+            e_t = psum_a.tile([P, width], F32, name="acc")
+            for c, cols in enumerate(blocks):
+                nc.tensor.matmul(e_t[:, cols], ref_i[:, cols], ident[:], start=(c == 0), stop=False, is_transpose=True)
+            for c, cols in enumerate(blocks):
+                nc.tensor.matmul(e_t[:, cols], neg[:, cols], ident[:], start=False, stop=(c == len(blocks) - 1),
+                                 is_transpose=True)
+            abs_t = work.tile([P, width], F32, name="w1")
+            nc.scalar.activation(abs_t[:], e_t[:], ACT.Abs)
+            e_abs = psum_c.tile([P, width], F32, name="acc")
+            for cols in blocks:
+                nc.tensor.transpose(e_abs[:, cols], abs_t[:, cols], ident[:])
+            y = work.tile([P, width], F32, name="w3")
+            nc.scalar.activation(y[:], e_abs[:], ACT.Sqrt, bias=one[:])
+            if i == len(pages):
+                page = page_pool.tile([P, T2], F32, name="page")
+                nc.gpsimd.memset(page[:], 0.0)
+                pages.append(page)
+            nc.vector.tensor_tensor(pages[i][:].indirect(list3[:, m0 // 16 : m1 // 16]), y[:], wgo_sb[:, m0:m1], ALU.mult)
+            if m1 == M:
+                nc.sync.dma_start(out_rows[b, t], pages[i][:])
+
         for mh in range(2):
-            x_codes, x_scales = x_q[mh]
-            for i in range(OUT_TILES):
-                b, t = divmod(i, PACK)
-                ref_i = ref_sb[b][:, t, mh * MH : (mh + 1) * MH]
-                acc = psum_b.tile([P, MH], F32, name="acc")
-                nc.tensor.matmul_mx(
-                    out=acc[:], lhsT=w4_q[:, 2 * i * P : 2 * (i + 1) * P].bitcast(FP4X4),
-                    lhsT_scale=w4_sc[:, i * P : (i + 1) * P],
-                    rhs=x_codes[:].bitcast(FP8X4), rhs_scale=x_scales[:], start=True, stop=True)
-                neg = work.tile([P, MH], F32, name="w0")
-                nc.scalar.activation(neg[:], acc[:], ACT.Copy, scale=-1.0)
-                e_t = psum_a.tile([P, MH], F32, name="acc")
-                for c, cols in enumerate(blocks):
-                    nc.tensor.matmul(e_t[:, cols], ref_i[:, cols], ident[:], start=(c == 0), stop=False, is_transpose=True)
-                for c, cols in enumerate(blocks):
-                    nc.tensor.matmul(e_t[:, cols], neg[:, cols], ident[:], start=False, stop=(c == len(blocks) - 1),
-                                     is_transpose=True)
-                abs_t = work.tile([P, MH], F32, name="w1")
-                nc.scalar.activation(abs_t[:], e_t[:], ACT.Abs)
-                e_abs = psum_c.tile([P, MH], F32, name="acc")
-                for cols in blocks:
-                    nc.tensor.transpose(e_abs[:, cols], abs_t[:, cols], ident[:])
-                y = work.tile([P, MH], F32, name="w3")
-                nc.scalar.activation(y[:], e_abs[:], ACT.Sqrt, bias=one[:])
-                nc.vector.tensor_tensor(pages[i][:].indirect(list3[:, mh * MH // 16 : (mh + 1) * MH // 16]), y[:],
-                                        wgo_sb[:, mh * MH : (mh + 1) * MH], ALU.mult)
-                if mh == 1:
-                    nc.sync.dma_start(out_rows[b, t], pages[i][:])
+            for i in range(SPLIT_TILES):
+                score(i, mh * MH, (mh + 1) * MH)
+        for i in range(SPLIT_TILES, OUT_TILES):
+            score(i, 0, M)

@@ -191,6 +191,9 @@ def tile_list_spirometry_obstruction_slots_kernel(
             nc.scalar.activation(s_shift[:], phase[:], ACT.Sin, scale=0.5, bias=quarter_pi[:])
             one_plus_sin = cos_pool.tile([P, BANK], F32, name="one_plus_sin")
             nc.scalar.activation(one_plus_sin[:], s_shift[:], ACT.Square, scale=math.sqrt(2.0))
+            if u == UNITS - 1:
+                warm = keep.tile([P, 1], F32, name="warm")
+                nc.scalar.activation(warm[:], one_plus_sin[:, 0:1], ACT.Sqrt, bias=one[:])
             neg_cos_d = stage.tile([P, BANK], F32, name="ncd%d" % u, align_bytes=64, offset=(56, 10, 20)[u % 3] * KIB)
             nc.vector.scalar_tensor_tensor(neg_cos_d[:], one_minus_cos[:], 1.0, d[:], ALU.subtract, ALU.mult)
             made[u] = (one_plus_sin, neg_cos_d)

import math
from contextlib import ExitStack

import concourse.mybir as mybir
from concourse.masks import make_identity

K, T, S, M, T2, H, N = 1024, 4096, 1024, 512, 1024, 512, 1024
FLOPS = 2 * (3 * K * H * S + H * N * M)

F32 = mybir.dt.float32
BF16 = mybir.dt.bfloat16
I32 = mybir.dt.int32
U32 = mybir.dt.uint32
U16 = mybir.dt.uint16
U8 = mybir.dt.uint8
FP8X4 = mybir.dt.float8_e4m3fn_x4
FP4X4 = mybir.dt.float4_e2m1fn_x4
ACT = mybir.ActivationFunctionType
ALU = mybir.AluOpType

P = 128
PACK = 4
K_PASS = P * PACK
PASSES = K // K_PASS
BANK = 512
HALVES = S // BANK
OUT_TILES = N // P
KIB = 1024
AHEAD = 2
W2_SCALAR_SHARE = 48
PAGE_BUFS = 4
SPLIT_TILES = 3
MH = M // 2
UNITS = PACK * HALVES


def tile_list_spirometry_obstruction_slots_kernel(
    tc, tab_words, tab_scales, offs, offs2, offs3, w1, w2, w3_words, w3_scales, wgt, bias,
    w4_words, w4_scales, ref, wgo, out,
):
    nc = tc.nc
    with ExitStack() as ctx:
        keep = ctx.enter_context(tc.tile_pool(name="keep", bufs=1))
        page_pool = ctx.enter_context(tc.tile_pool(name="pages", bufs=PAGE_BUFS))
        stage = ctx.enter_context(tc.tile_pool(name="stage", bufs=1))
        work = ctx.enter_context(tc.tile_pool(name="work", bufs=3))
        cos_pool = ctx.enter_context(tc.tile_pool(name="cosd", bufs=4))
        psum_a = ctx.enter_context(tc.psum_pool(name="psum_a", bufs=3))
        psum_b = ctx.enter_context(tc.psum_pool(name="psum_b", bufs=3))
        psum_c = ctx.enter_context(tc.psum_pool(name="psum_c", bufs=2))

        tab_sc = stage.tile([P, T], U8, name="tab_sc", align_bytes=64, offset=32 * KIB)
        w3_sc_raw = keep.tile([P, H], U8, name="w3_sc_raw", align_bytes=64)
        w4_sc_raw = keep.tile([P, N], U8, name="w4_sc_raw", align_bytes=64)
        for plane in (tab_sc, w4_sc_raw, w3_sc_raw):
            nc.vector.memset(plane[:].bitcast(I32), 0)

        list1 = keep.tile([P, S // 16], U16, name="list1")
        nc.sync.dma_start(list1[:], offs)
        tab = [stage.tile([P, T], U32, name="tab%d" % a, align_bytes=64, offset=16 * KIB * a) for a in range(PASSES)]

        def load_tab(a):
            nc.sync.dma_start(tab[a][:].bitcast(I32), tab_words[a].rearrange("p t i -> p (t i)").bitcast(I32))

        def load_raw(w, a, offset):
            tile = stage.tile([P, PACK, H], F32, name="raw%d" % (offset // KIB), align_bytes=64, offset=offset)
            nc.sync.dma_start(tile[:], w[a * K_PASS : (a + 1) * K_PASS, :].rearrange("(p j) c -> p j c", j=PACK))
            return tile

        def load_planes(plane, scales):
            for q in range(4):
                nc.sync.dma_start(plane[32 * q : 32 * q + 4 * scales.shape[0], :].bitcast(I32),
                                scales[:, 4 * q : 4 * q + 4, :].bitcast(I32))

        load_tab(0)
        load_planes(tab_sc, tab_scales)
        w1_raw = [load_raw(w1, a, (40 + 8 * a) * KIB) for a in range(PASSES)]
        w4_raw = keep.tile([P, 2 * N], U8, name="w4_raw", align_bytes=64)
        nc.sync.dma_start(w4_raw[:].bitcast(I32), w4_words[0].bitcast(I32))
        load_planes(w4_sc_raw, w4_scales)
        load_tab(1)
        load_planes(w3_sc_raw, w3_scales)
        w3_raw = keep.tile([P, PASSES, H], I32, name="w3_raw", align_bytes=64)
        nc.sync.dma_start(w3_raw[:], w3_words.rearrange("a p c i -> p a (c i)").bitcast(I32))
        w2_raw = [load_raw(w2, a, (56 + 8 * a) * KIB) for a in range(PASSES)]

        list2 = keep.tile([P, M // 16], U16, name="list2")
        nc.sync.dma_start(list2[:], offs2)
        wgt_sb = keep.tile([P, M], F32, name="wgt_sb")
        nc.sync.dma_start(wgt_sb[:], wgt)
        bias_sb = keep.tile([P, PACK], F32, name="bias_sb")
        nc.sync.dma_start(bias_sb[:], bias.rearrange("(p t) -> p t", t=PACK))
        list3 = keep.tile([P, M // 16], U16, name="list3")
        nc.sync.dma_start(list3[:], offs3)
        wgo_sb = keep.tile([P, M], F32, name="wgo_sb")
        nc.sync.dma_start(wgo_sb[:], wgo)

        ident = keep.tile([P, P], F32, name="ident")
        make_identity(nc, ident[:])
        one = keep.tile([P, 1], F32, name="one")
        nc.vector.memset(one[:], 1.0)
        quarter_pi = keep.tile([P, 1], F32, name="quarter_pi")
        nc.vector.tensor_scalar(quarter_pi[:], one[:], math.pi / 4, None, ALU.mult)

        pages = []
        for i in range(PAGE_BUFS):
            page = page_pool.tile([P, T2], F32, name="page")
            nc.vector.memset(page[:], 0.0)
            pages.append(page)

        w4_q = keep.tile([P, 2 * N], U8, name="w4_q", align_bytes=64)
        nc.vector.tensor_copy(
            w4_q[:].bitcast(U16).rearrange("p (b t q) -> p b t q", t=PACK, q=P),
            w4_raw[:].bitcast(U16).rearrange("p (b q t) -> p b t q", t=PACK, q=P))


        v = [[None] * HALVES for a in range(PASSES)]

        def gather_words(a):
            for jh in range(HALVES):
                tile = keep.tile([P, BANK], U32, name="v%d_%d" % (a, jh), align_bytes=64)
                nc.vector.tensor_copy(tile[:], tab[a][:].indirect(list1[:, jh * BANK // 16 : (jh + 1) * BANK // 16]))
                v[a][jh] = tile

        def quantise(raw, name, offset, scalar_share):
            grouped = stage.tile([P, PACK * H], BF16, name=name + "_grouped", align_bytes=64, offset=offset)
            dealt = grouped[:].rearrange("p (t q j) -> p q t j", t=PACK, j=PACK)
            rows = raw[:].rearrange("p j (q t) -> p q t j", t=PACK)
            if scalar_share > 0:
                nc.scalar.copy(dealt[:, :scalar_share], rows[:, :scalar_share])
            if scalar_share < P:
                nc.vector.tensor_copy(dealt[:, scalar_share:], rows[:, scalar_share:])
            codes = keep.tile([P, H], U32, name=name + "_codes", align_bytes=64)
            scales = keep.tile([P, H], U8, name=name + "_scales", align_bytes=64)
            nc.vector.quantize_mx(codes[:].bitcast(FP8X4), scales[:], grouped[:])
            return codes[:], scales[:]

        gather_words(0)
        v_sc = keep.tile([P, S], U8, name="v_sc", align_bytes=64)
        nc.vector.tensor_copy(v_sc[:], tab_sc[:].indirect(list1[:]))
        w4_sc = stage.tile([P, N], U8, name="w4_sc", align_bytes=64, offset=KIB)
        nc.vector.tensor_copy(w4_sc[:].rearrange("p (b t q) -> p b t q", t=PACK, q=P),
                              w4_sc_raw[:].rearrange("p (b q t) -> p b t q", t=PACK, q=P))
        w1_q = [quantise(w1_raw[0], "w1_0", 36 * KIB, P),
                quantise(w1_raw[1], "w1_1", 32 * KIB, P // 2)]
        gather_words(1)
        w3_sc = stage.tile([P, H], U8, name="w3_sc", align_bytes=64, offset=0)
        nc.vector.tensor_copy(w3_sc[:].rearrange("p (t q) -> p t q", t=PACK),
                              w3_sc_raw[:].rearrange("p (q t) -> p t q", t=PACK))
        w3_codes = stage.tile([P, PASSES, H], I32, name="w3_codes", align_bytes=64, offset=16 * KIB)
        nc.vector.tensor_copy(w3_codes[:].rearrange("p a (t q) -> p a q t", t=PACK),
                              w3_raw[:].rearrange("p a (q t) -> p a q t", t=PACK))
        w3_q = [(w3_codes[:, a, :], w3_sc[4 * a :, :]) for a in range(PASSES)]

        ref_sb = []
        for b in range(N // K_PASS):
            tile = stage.tile([P, PACK, M], F32, name="ref%d" % b, align_bytes=64, offset=(2 + 22 * b) * KIB)
            nc.sync.dma_start(tile[:], ref[b * K_PASS : (b + 1) * K_PASS, :].rearrange("(p t) m -> p t m", t=PACK))
            ref_sb.append(tile)

        def product(pool, w_q, t, jh):
            acc = pool.tile([P, BANK], F32, name="acc")
            for a in range(PASSES):
                codes, scales = w_q[a]
                nc.tensor.matmul_mx(
                    out=acc[:], lhsT=codes[:, t * P : (t + 1) * P].bitcast(FP8X4), lhsT_scale=scales[:, t * P : (t + 1) * P],
                    rhs=v[a][jh][:].bitcast(FP8X4), rhs_scale=v_sc[4 * a :, jh * BANK : (jh + 1) * BANK],
                    start=(a == 0), stop=(a == PASSES - 1))
            return acc

        x_rows = [keep.tile([P, PACK * MH], BF16, name="x_rows%d" % mh, align_bytes=64) for mh in range(2)]
        h = [keep.tile([P, S], F32, name="h%d" % t) for t in range(PACK)]
        w2_q = [quantise(w2_raw[a], "w2_%d" % a, (10 + 10 * a) * KIB, W2_SCALAR_SHARE) for a in range(PASSES)]
        made = {}

        def front(u):
            t, jh = divmod(u, HALVES)
            phase = product(psum_a, w1_q, t, jh)
            d = product(psum_c, w3_q, t, jh)
            held = [125 * KIB // 2 + 2 * KIB * slot for slot in range(5)]
            s_half = stage.tile([P, BANK], F32, name="s_half%d" % u, align_bytes=64,
                                offset=(40 * KIB, 58 * KIB)[u] if u < 2 else held[u % 2])
            nc.scalar.activation(s_half[:], phase[:], ACT.Sin, scale=0.5)
            if u == 1:
                one_minus_cos = stage.tile([P, BANK], F32, name="omc%d" % u, align_bytes=64, offset=held[4])
            else:
                one_minus_cos = work.tile([P, BANK], F32, name="w2")
            nc.scalar.activation(one_minus_cos[:], s_half[:], ACT.Square, scale=math.sqrt(2.0))
            s_shift = stage.tile([P, BANK], F32, name="s_shift%d" % u, align_bytes=64,
                                 offset=42 * KIB if u == 0 else held[2 + u % 2])
            nc.scalar.activation(s_shift[:], phase[:], ACT.Sin, scale=0.5, bias=quarter_pi[:])
            one_plus_sin = cos_pool.tile([P, BANK], F32, name="one_plus_sin")
            nc.scalar.activation(one_plus_sin[:], s_shift[:], ACT.Square, scale=math.sqrt(2.0))
            if u == UNITS - 1:
                warm = keep.tile([P, 1], F32, name="warm")
                nc.scalar.activation(warm[:], one_plus_sin[:, 0:1], ACT.Sqrt, bias=one[:])
            neg_cos_d = stage.tile([P, BANK], F32, name="ncd%d" % u, align_bytes=64, offset=(56, 10, 20)[u % 3] * KIB)
            nc.vector.scalar_tensor_tensor(neg_cos_d[:], one_minus_cos[:], 1.0, d[:], ALU.subtract, ALU.mult)
            made[u] = (one_plus_sin, neg_cos_d)

        def pick(t, mh, picked):
            nc.vector.tensor_tensor(picked[:], h[t][:].indirect(list2[:, mh * MH // 16 : (mh + 1) * MH // 16]),
                                    wgt_sb[:, mh * MH : (mh + 1) * MH], ALU.mult)
            nc.scalar.activation(x_rows[mh][:, t * MH : (t + 1) * MH], picked[:], ACT.Identity, bias=bias_sb[:, t : t + 1])

        def back(u):
            t, jh = divmod(u, HALVES)
            one_plus_sin, neg_cos_d = made[u]
            b = product(psum_b, w2_q, t, jh)
            if u == UNITS - 1:
                sin_b = stage.tile([P, BANK], F32, name="sin_b_last", align_bytes=64, offset=36 * KIB)
            else:
                sin_b = work.tile([P, BANK], F32, name="w4")
            nc.vector.scalar_tensor_tensor(sin_b[:], one_plus_sin[:], 1.0, b[:], ALU.subtract, ALU.mult)
            nc.vector.scalar_tensor_tensor(h[t][:, jh * BANK : (jh + 1) * BANK], neg_cos_d[:], -1.0, sin_b[:],
                                           ALU.mult, ALU.max)
            if jh == HALVES - 1:
                picked = work.tile([P, MH], F32, name="w5")
                pick(t, 0, picked)

        for u in range(UNITS + AHEAD):
            if u < UNITS:
                front(u)
            if u >= AHEAD:
                back(u - AHEAD)

        x_codes = keep.tile([P, M], U32, name="x_codes", align_bytes=64)
        x_scales = keep.tile([P, M], U8, name="x_scales", align_bytes=64)

        def quantise_x(mh, offset):
            grouped = stage.tile([P, PACK * MH], BF16, name="x_grouped%d" % mh, align_bytes=64, offset=offset)
            nc.vector.tensor_copy(grouped[:].rearrange("p (c i t) -> p c t i", i=4, t=PACK),
                                  x_rows[mh][:].rearrange("p (t c i) -> p c t i", i=4, t=PACK))
            cols = slice(mh * MH, (mh + 1) * MH)
            nc.vector.quantize_mx(x_codes[:, cols].bitcast(FP8X4), x_scales[:, cols], grouped[:])

        quantise_x(0, 33 * KIB)
        for t in range(PACK):
            offset = 36 * KIB if t == 0 else (32 + t) * KIB - KIB // 2
            picked = stage.tile([P, MH], F32, name="picked%d" % t, align_bytes=64, offset=offset)
            pick(t, 1, picked)
        quantise_x(1, 38 * KIB)

        out_rows = out.rearrange("(b p t) c -> b t p c", p=P, t=PACK)

        def score(i, m0, m1):
            b, t = divmod(i, PACK)
            width = m1 - m0
            blocks = [slice(c * P, (c + 1) * P) for c in range(width // P)]
            ref_i = ref_sb[b][:, t, m0:m1]
            acc = psum_b.tile([P, width], F32, name="acc")
            nc.tensor.matmul_mx(
                out=acc[:], lhsT=w4_q[:, 2 * i * P : 2 * (i + 1) * P].bitcast(FP4X4),
                lhsT_scale=w4_sc[:, i * P : (i + 1) * P],
                rhs=x_codes[:, m0:m1].bitcast(FP8X4), rhs_scale=x_scales[:, m0:m1], start=True, stop=True)
            neg = work.tile([P, width], F32, name="w0")
            nc.scalar.activation(neg[:], acc[:], ACT.Copy, scale=-1.0)
            e_t = psum_a.tile([P, width], F32, name="acc")
            for c, cols in enumerate(blocks):
                nc.tensor.matmul(e_t[:, cols], ref_i[:, cols], ident[:], start=(c == 0), stop=False, is_transpose=True)
            for c, cols in enumerate(blocks):
                nc.tensor.matmul(e_t[:, cols], neg[:, cols], ident[:], start=False, stop=(c == len(blocks) - 1),
                                 is_transpose=True)
            abs_t = work.tile([P, width], F32, name="w1")
            nc.scalar.activation(abs_t[:], e_t[:], ACT.Abs)
            e_abs = psum_c.tile([P, width], F32, name="acc")
            for cols in blocks:
                nc.tensor.transpose(e_abs[:, cols], abs_t[:, cols], ident[:])
            y = work.tile([P, width], F32, name="w3")
            nc.scalar.activation(y[:], e_abs[:], ACT.Sqrt, bias=one[:])
            if i == len(pages):
                page = page_pool.tile([P, T2], F32, name="page")
                nc.gpsimd.memset(page[:], 0.0)
                pages.append(page)
            nc.vector.tensor_tensor(pages[i][:].indirect(list3[:, m0 // 16 : m1 // 16]), y[:], wgo_sb[:, m0:m1], ALU.mult)
            if m1 == M:
                nc.sync.dma_start(out_rows[b, t], pages[i][:])

        for mh in range(2):
            for i in range(SPLIT_TILES):
                score(i, mh * MH, (mh + 1) * MH)
        for i in range(SPLIT_TILES, OUT_TILES):
            score(i, 0, M)
